import numpy as np
import ml_dtypes

BF16 = ml_dtypes.bfloat16


def bf(x):
    return np.asarray(x, np.float32).astype(BF16)


def f32(x):
    return np.asarray(x, np.float32)


def f64(x):
    return np.asarray(x).astype(np.float64)


def striped(idx):
    return np.tile(idx.reshape(-1, 16).T, (8, 1))


S, K, M, N, E, Q = 512, 128, 128, 384, 2, 192


def gelu_tanh(v):
    return 0.5 * v * (1.0 + np.tanh(np.sqrt(2.0 / np.pi) * (v + 0.044715 * v**3)))


def setup_inputs():
    return {"base": bf(np.random.standard_normal((M, S))), "x": bf(np.random.standard_normal((K, N))), "w": bf(np.random.standard_normal((E, K, M)) / np.sqrt(K)), "b": f32(0.5 * np.random.standard_normal((M, 1))), "offs": striped(np.random.permutation(S)[:N])}


def reference(base, x, w, b, offs):
    idx = offs[:16].T.reshape(-1)
    z = f64(base).copy()
    for e in range(E):
        z[:, idx[e * Q : (e + 1) * Q]] = f64(w)[e].T @ f64(x)[:, e * Q : (e + 1) * Q]
    return gelu_tanh(z + f64(b))

@@ -1,0 +1,52 @@
+import concourse.mybir as mybir
+from concourse.masks import make_identity
+
+BF16, F32, U16 = mybir.dt.bfloat16, mybir.dt.float32, mybir.dt.uint16
+GELU_TANH = mybir.ActivationFunctionType.Gelu_apprx_tanh
+
+P = 128
+S = 512
+N = 384
+E = 2
+Q = N // E
+OFFSETS_PER_COLUMN = 16
+
+FLOPS = 2 * P * P * N
+
+
+def tile_scatter_matmul_kernel(tc, base, x, w, b, offs, out):
+    nc = tc.nc
+    with (
+        tc.tile_pool(name="held", bufs=1) as held,
+        tc.psum_pool(name="psum", bufs=1) as psum,
+    ):
+        offsets = held.tile([P, N // OFFSETS_PER_COLUMN], U16, name="offsets")
+        nc.sync.dma_start(offsets[:], offs)
+        base_tile = held.tile([P, S], BF16, name="base_tile")
+        nc.scalar.dma_start(base_tile[:], base)
+        x_tile = held.tile([P, N], BF16, name="x_tile")
+        nc.sync.dma_start(x_tile[:], x)
+        w_tile = held.tile([P, E, P], BF16, name="w_tile")
+        nc.scalar.dma_start(w_tile[:], w.rearrange("e k m -> k e m"))
+        bias = held.tile([P, 1], F32, name="bias")
+        nc.gpsimd.dma_start(bias[:], b)
+
+        identity = held.tile([P, P], BF16, name="identity")
+        make_identity(nc, identity[:])
+
+        window = psum.tile([P, S], F32, name="window")
+        nc.tensor.matmul(window[:], identity[:], base_tile[:], start=True, stop=True)
+
+        for e in range(E):
+            piece = offsets[:, e * Q // OFFSETS_PER_COLUMN : (e + 1) * Q // OFFSETS_PER_COLUMN]
+            nc.tensor.matmul(
+                window[:].indirect(piece),
+                w_tile[:, e, :],
+                x_tile[:, e * Q : (e + 1) * Q],
+                start=True,
+                stop=True,
+            )
+
+        result = held.tile([P, S], F32, name="result")
+        nc.scalar.activation(result[:], window[:], GELU_TANH, bias=bias[:])
+        nc.sync.dma_start(out, result[:])

@@ -29,7 +29,11 @@ def tile_scatter_matmul_kernel(tc, base, x, w, b, offs, out):
         w_tile = held.tile([P, E, P], BF16, name="w_tile")
         nc.scalar.dma_start(w_tile[:], w.rearrange("e k m -> k e m"))
         bias = held.tile([P, 1], F32, name="bias")
-        nc.gpsimd.dma_start(bias[:], b)
+        nc.sync.dma_start(bias[:], b)
+
+        scratch = held.tile([P, 1], F32, name="scratch")
+        nc.vector.memset(scratch[:], 0.0)
+        nc.scalar.activation(scratch[:], scratch[:], GELU_TANH)
 
         identity = held.tile([P, P], BF16, name="identity")
         make_identity(nc, identity[:])

@@ -9,6 +9,7 @@ S = 512
 N = 384
 E = 2
 Q = N // E
+HALF = S // 2
 OFFSETS_PER_COLUMN = 16
 
 FLOPS = 2 * P * P * N
@@ -52,5 +53,7 @@ def tile_scatter_matmul_kernel(tc, base, x, w, b, offs, out):
             )
 
         result = held.tile([P, S], F32, name="result")
-        nc.scalar.activation(result[:], window[:], GELU_TANH, bias=bias[:])
-        nc.sync.dma_start(out, result[:])
+        for half, queue in enumerate((nc.sync, nc.scalar)):
+            columns = slice(half * HALF, (half + 1) * HALF)
+            nc.scalar.activation(result[:, columns], window[:, columns], GELU_TANH, bias=bias[:])
+            queue.dma_start(out[:, columns], result[:, columns])

@@ -9,7 +9,7 @@ S = 512
 N = 384
 E = 2
 Q = N // E
-HALF = S // 2
+WARMING_MATMULS = 3
 OFFSETS_PER_COLUMN = 16
 
 FLOPS = 2 * P * P * N
@@ -32,9 +32,13 @@ def tile_scatter_matmul_kernel(tc, base, x, w, b, offs, out):
         bias = held.tile([P, 1], F32, name="bias")
         nc.sync.dma_start(bias[:], b)
 
+        zeros = held.tile([P, S], BF16, name="zeros")
+        nc.vector.memset(zeros[:], 0.0)
         scratch = held.tile([P, 1], F32, name="scratch")
-        nc.vector.memset(scratch[:], 0.0)
-        nc.scalar.activation(scratch[:], scratch[:], GELU_TANH)
+        nc.scalar.activation(scratch[:], zeros[:, 0:1], GELU_TANH)
+        unread = psum.tile([P, S], F32, name="unread")
+        for _ in range(WARMING_MATMULS):
+            nc.tensor.matmul(unread[:], zeros[:, 0:P], zeros[:], start=True, stop=True)
 
         identity = held.tile([P, P], BF16, name="identity")
         make_identity(nc, identity[:])
@@ -53,7 +57,5 @@ def tile_scatter_matmul_kernel(tc, base, x, w, b, offs, out):
             )
 
         result = held.tile([P, S], F32, name="result")
-        for half, queue in enumerate((nc.sync, nc.scalar)):
-            columns = slice(half * HALF, (half + 1) * HALF)
-            nc.scalar.activation(result[:, columns], window[:, columns], GELU_TANH, bias=bias[:])
-            queue.dma_start(out[:, columns], result[:, columns])
+        nc.scalar.activation(result[:], window[:], GELU_TANH, bias=bias[:])
+        nc.sync.dma_start(out, result[:])

@@ -21,14 +21,14 @@ def tile_scatter_matmul_kernel(tc, base, x, w, b, offs, out):
         tc.tile_pool(name="held", bufs=1) as held,
         tc.psum_pool(name="psum", bufs=1) as psum,
     ):
+        base_tile = held.tile([P, S], BF16, name="base_tile")
+        nc.sync.dma_start(base_tile[:], base)
         offsets = held.tile([P, N // OFFSETS_PER_COLUMN], U16, name="offsets")
         nc.sync.dma_start(offsets[:], offs)
-        base_tile = held.tile([P, S], BF16, name="base_tile")
-        nc.scalar.dma_start(base_tile[:], base)
         x_tile = held.tile([P, N], BF16, name="x_tile")
         nc.sync.dma_start(x_tile[:], x)
         w_tile = held.tile([P, E, P], BF16, name="w_tile")
-        nc.scalar.dma_start(w_tile[:], w.rearrange("e k m -> k e m"))
+        nc.sync.dma_start(w_tile[:], w.rearrange("e k m -> k e m"))
         bias = held.tile([P, 1], F32, name="bias")
         nc.sync.dma_start(bias[:], b)
 

@@ -25,10 +25,11 @@ def tile_scatter_matmul_kernel(tc, base, x, w, b, offs, out):
         nc.sync.dma_start(base_tile[:], base)
         offsets = held.tile([P, N // OFFSETS_PER_COLUMN], U16, name="offsets")
         nc.sync.dma_start(offsets[:], offs)
-        x_tile = held.tile([P, N], BF16, name="x_tile")
-        nc.sync.dma_start(x_tile[:], x)
-        w_tile = held.tile([P, E, P], BF16, name="w_tile")
-        nc.sync.dma_start(w_tile[:], w.rearrange("e k m -> k e m"))
+        w_tiles = [held.tile([P, P], BF16, name=f"w_tile{e}") for e in range(E)]
+        x_tiles = [held.tile([P, Q], BF16, name=f"x_tile{e}") for e in range(E)]
+        for e in range(E):
+            nc.sync.dma_start(w_tiles[e][:], w[e])
+            nc.sync.dma_start(x_tiles[e][:], x[:, e * Q : (e + 1) * Q])
         bias = held.tile([P, 1], F32, name="bias")
         nc.sync.dma_start(bias[:], b)
 
@@ -50,8 +51,8 @@ def tile_scatter_matmul_kernel(tc, base, x, w, b, offs, out):
             piece = offsets[:, e * Q // OFFSETS_PER_COLUMN : (e + 1) * Q // OFFSETS_PER_COLUMN]
             nc.tensor.matmul(
                 window[:].indirect(piece),
-                w_tile[:, e, :],
-                x_tile[:, e * Q : (e + 1) * Q],
+                w_tiles[e][:],
+                x_tiles[e][:],
                 start=True,
                 stop=True,
             )

@@ -9,7 +9,7 @@ S = 512
 N = 384
 E = 2
 Q = N // E
-WARMING_MATMULS = 3
+WARMING_MATMULS = 2
 OFFSETS_PER_COLUMN = 16
 
 FLOPS = 2 * P * P * N

@@ -10,6 +10,7 @@ N = 384
 E = 2
 Q = N // E
 WARMING_MATMULS = 2
+REPEATS = S // P
 OFFSETS_PER_COLUMN = 16
 
 FLOPS = 2 * P * P * N
@@ -33,13 +34,20 @@ def tile_scatter_matmul_kernel(tc, base, x, w, b, offs, out):
         bias = held.tile([P, 1], F32, name="bias")
         nc.sync.dma_start(bias[:], b)
 
-        zeros = held.tile([P, S], BF16, name="zeros")
+        zeros = held.tile([P, P], BF16, name="zeros")
         nc.vector.memset(zeros[:], 0.0)
         scratch = held.tile([P, 1], F32, name="scratch")
         nc.scalar.activation(scratch[:], zeros[:, 0:1], GELU_TANH)
         unread = psum.tile([P, S], F32, name="unread")
+        zeros_repeated = zeros[:].unsqueeze(1).to_broadcast([P, REPEATS, P])
         for _ in range(WARMING_MATMULS):
-            nc.tensor.matmul(unread[:], zeros[:, 0:P], zeros[:], start=True, stop=True)
+            nc.tensor.matmul(
+                unread[:].rearrange("p (r c) -> p r c", r=REPEATS),
+                zeros[:],
+                zeros_repeated,
+                start=True,
+                stop=True,
+            )
 
         identity = held.tile([P, P], BF16, name="identity")
         make_identity(nc, identity[:])

@@ -9,8 +9,8 @@ S = 512
 N = 384
 E = 2
 Q = N // E
-WARMING_MATMULS = 2
-REPEATS = S // P
+WARMING_MATMULS = 3
+REPEATS = 3
 OFFSETS_PER_COLUMN = 16
 
 FLOPS = 2 * P * P * N
@@ -38,11 +38,11 @@ def tile_scatter_matmul_kernel(tc, base, x, w, b, offs, out):
         nc.vector.memset(zeros[:], 0.0)
         scratch = held.tile([P, 1], F32, name="scratch")
         nc.scalar.activation(scratch[:], zeros[:, 0:1], GELU_TANH)
-        unread = psum.tile([P, S], F32, name="unread")
+        unread = psum.tile([P, REPEATS, P], F32, name="unread")
         zeros_repeated = zeros[:].unsqueeze(1).to_broadcast([P, REPEATS, P])
         for _ in range(WARMING_MATMULS):
             nc.tensor.matmul(
-                unread[:].rearrange("p (r c) -> p r c", r=REPEATS),
+                unread[:],
                 zeros[:],
                 zeros_repeated,
                 start=True,

import concourse.mybir as mybir
from concourse.masks import make_identity

BF16, F32, U16 = mybir.dt.bfloat16, mybir.dt.float32, mybir.dt.uint16
GELU_TANH = mybir.ActivationFunctionType.Gelu_apprx_tanh

P = 128
S = 512
N = 384
E = 2
Q = N // E
WARMING_MATMULS = 3
REPEATS = 3
OFFSETS_PER_COLUMN = 16

FLOPS = 2 * P * P * N


def tile_scatter_matmul_kernel(tc, base, x, w, b, offs, out):
    nc = tc.nc
    with (
        tc.tile_pool(name="held", bufs=1) as held,
        tc.psum_pool(name="psum", bufs=1) as psum,
    ):
        base_tile = held.tile([P, S], BF16, name="base_tile")
        nc.sync.dma_start(base_tile[:], base)
        offsets = held.tile([P, N // OFFSETS_PER_COLUMN], U16, name="offsets")
        nc.sync.dma_start(offsets[:], offs)
        w_tiles = [held.tile([P, P], BF16, name=f"w_tile{e}") for e in range(E)]
        x_tiles = [held.tile([P, Q], BF16, name=f"x_tile{e}") for e in range(E)]
        for e in range(E):
            nc.sync.dma_start(w_tiles[e][:], w[e])
            nc.sync.dma_start(x_tiles[e][:], x[:, e * Q : (e + 1) * Q])
        bias = held.tile([P, 1], F32, name="bias")
        nc.sync.dma_start(bias[:], b)

        zeros = held.tile([P, P], BF16, name="zeros")
        nc.vector.memset(zeros[:], 0.0)
        scratch = held.tile([P, 1], F32, name="scratch")
        nc.scalar.activation(scratch[:], zeros[:, 0:1], GELU_TANH)
        unread = psum.tile([P, REPEATS, P], F32, name="unread")
        zeros_repeated = zeros[:].unsqueeze(1).to_broadcast([P, REPEATS, P])
        for _ in range(WARMING_MATMULS):
            nc.tensor.matmul(
                unread[:],
                zeros[:],
                zeros_repeated,
                start=True,
                stop=True,
            )

        identity = held.tile([P, P], BF16, name="identity")
        make_identity(nc, identity[:])

        window = psum.tile([P, S], F32, name="window")
        nc.tensor.matmul(window[:], identity[:], base_tile[:], start=True, stop=True)

        for e in range(E):
            piece = offsets[:, e * Q // OFFSETS_PER_COLUMN : (e + 1) * Q // OFFSETS_PER_COLUMN]
            nc.tensor.matmul(
                window[:].indirect(piece),
                w_tiles[e][:],
                x_tiles[e][:],
                start=True,
                stop=True,
            )

        result = held.tile([P, S], F32, name="result")
        nc.scalar.activation(result[:], window[:], GELU_TANH, bias=bias[:])
        nc.sync.dma_start(out, result[:])
